import numpy as np
import ml_dtypes


def mxq(x, axis, fmt="e4m3"):
    dtype, down = {"e4m3": (ml_dtypes.float8_e4m3fn, 7), "e5m2": (ml_dtypes.float8_e5m2, 14)}[fmt]
    v = np.moveaxis(np.asarray(x, np.float32).astype(ml_dtypes.bfloat16).astype(np.float64), axis, -1)
    blocks = v.reshape(v.shape[:-1] + (-1, 32))
    amax = np.abs(blocks).max(-1, keepdims=True)
    byte = np.maximum(np.where(amax > 0, np.frexp(amax)[1] - 1 + 127, 0) - down, 1)
    scale = np.exp2(byte - 127.0)
    codes = (blocks / scale).astype(np.float32).astype(dtype).astype(np.float64)
    return np.moveaxis((codes * scale).reshape(v.shape), -1, axis)


WIDE = False


def mx_kscale(k):
    if not WIDE:
        return np.ones(k)
    levels = np.array([10, -10, 5, -5, 0])
    if k % 512:
        return np.exp2(np.random.permutation(np.resize(levels, k // 32))).repeat(32)
    a = np.empty((k // 512, 16))
    for p in range(k // 512):
        a[p, :8] = np.random.permutation(np.resize(levels, 8))
        for g in range(8):
            far = levels[np.abs(levels - a[p, g]) >= 10]
            a[p, g + 8] = far[np.random.randint(len(far))]
    return np.exp2(a.ravel()).repeat(32)


def f64(x):
    return np.asarray(x).astype(np.float64)


E2M1 = np.array([0.0, 0.5, 1.0, 1.5, 2.0, 3.0, 4.0, 6.0, -0.0, -0.5, -1.0, -1.5, -2.0, -3.0, -4.0, -6.0])


def pack_weight(w, fmt):
    k, n = w.shape
    w = f64(np.asarray(w, np.float32).astype(ml_dtypes.bfloat16)).reshape(k // 32, 32, n)
    amax = np.abs(w).max(1)
    if fmt == "e4m3":
        byte = np.frexp(amax)[1] - 1 + 127 - 7
    else:
        mant, ex = np.frexp(amax / 6.0)
        byte = np.where(mant > 0.5, ex, ex - 1) + 127
    byte = np.clip(np.where(amax > 0, byte, 1), 1, 254)
    scaled = (w * np.exp2(127.0 - byte)[:, None, :]).reshape(k, n).astype(np.float32)
    by_word = np.ascontiguousarray(scaled.reshape(k // 512, 128, 4, n).transpose(0, 1, 3, 2))
    if fmt == "e4m3":
        words = by_word.astype(ml_dtypes.float8_e4m3fn).view(np.uint8)
    else:
        c = by_word.astype(ml_dtypes.float4_e2m1fn).view(np.uint8) & 0xF
        words = (c[..., 0::2] | (c[..., 1::2] << 4)).reshape(k // 512, 128, 2 * n)
    return np.ascontiguousarray(words), np.ascontiguousarray(byte.astype(np.uint8).reshape(k // 512, 16, n))


def unpack_weight(words, scales, fmt):
    g, _, n = scales.shape
    words = np.ascontiguousarray(words).reshape(g, 128, n, -1)
    if fmt == "e4m3":
        vals = words.view(ml_dtypes.float8_e4m3fn).astype(np.float64)
    else:
        nib = np.empty((g, 128, n, 4), np.uint8)
        nib[..., 0::2] = words & 0xF
        nib[..., 1::2] = words >> 4
        vals = E2M1[nib]
    vals = vals * np.repeat(np.exp2(scales.astype(np.float64) - 127.0), 8, axis=1)[..., None]
    return vals.transpose(0, 1, 3, 2).reshape(g * 512, n)


K, M, T = 1024, 1536, 1536


def setup_inputs():
    n = np.random.standard_normal
    s = mx_kscale(K)[:, None]
    p_w4 = pack_weight(n((K, M)) / np.sqrt(K) / s, "e2m1")
    p_w8 = pack_weight(n((K, M)) / np.sqrt(K) / s, "e4m3")
    return {
        "x": (n((K, T)) * s).astype(np.float32),
        "w4_words": p_w4[0],
        "w4_scales": p_w4[1],
        "w8_words": p_w8[0],
        "w8_scales": p_w8[1],
        "b": (0.3 * n(1536)).astype(np.float32),
    }


def reference(x, w4_words, w4_scales, w8_words, w8_scales, b):
    xa_, xb_ = mxq(np.maximum(f64(x), 0.0), 0, "e4m3"), mxq(np.maximum(-f64(x), 0.0), 0, "e4m3")
    w4_ = unpack_weight(w4_words, w4_scales, "e2m1")
    w8_ = unpack_weight(w8_words, w8_scales, "e4m3")
    y = xa_.T @ w4_ + xb_.T @ w8_
    return y + f64(b)[None, :]

@@ -1,0 +1,230 @@
+from contextlib import ExitStack
+
+import concourse.mybir as mybir
+from concourse.masks import make_identity
+
+K, M, T = 1024, 1536, 1536
+FLOPS = 2 * 2 * K * M * T
+
+F32 = mybir.dt.float32
+BF16 = mybir.dt.bfloat16
+I32 = mybir.dt.int32
+U32 = mybir.dt.uint32
+U8 = mybir.dt.uint8
+E4M3 = mybir.dt.float8_e4m3fn_x4
+E2M1 = mybir.dt.float4_e2m1fn_x4
+ALU = mybir.AluOpType
+RELU = mybir.ActivationFunctionType.Relu
+
+P = 128
+PACK = 4
+K_PASS = P * PACK
+PASSES = K // K_PASS
+NB = 512
+N_BLOCKS = M // NB
+T_TILES = T // P
+BANKS = 8
+HEAD = 4
+POS, NEG = 0, 1
+UNITS = [(a, f) for a in range(PASSES) for f in (POS, NEG)]
+W8_ROW = 4
+
+
+def tile_mix_feat_tm_crelu_bias_kernel(tc, x, w4_words, w4_scales, w8_words, w8_scales, b, out):
+    nc = tc.nc
+    with ExitStack() as ctx:
+        keep = ctx.enter_context(tc.tile_pool(name="keep", bufs=1))
+        stage = ctx.enter_context(tc.tile_pool(name="stage", bufs=6))
+        psum = ctx.enter_context(tc.psum_pool(name="psum", bufs=1))
+        ctx.enter_context(tc.manual_schedule())
+
+        raw = {}
+        weights = {}
+        grouped = {}
+        codes = {}
+        scales = {}
+        acc = {}
+        result = {}
+
+        plane4 = keep.tile([P, PASSES, M], U8, name="plane4", align_bytes=64)
+        plane8 = keep.tile([P, PASSES, M], U8, name="plane8", align_bytes=64)
+        zero_in = keep.tile([P, 1], F32, name="zero_in")
+        zero = keep.tile([P, 1], F32, name="zero")
+        ident = keep.tile([P, P], F32, name="ident")
+        b_cols = keep.tile([P, N_BLOCKS, PACK], F32, name="b_cols")
+
+        nc.vector.memset(zero_in[:], 0.0)
+        nc.scalar.activation(out=zero[:], in_=zero_in[:], func=RELU, bias=zero_in[:])
+        nc.vector.memset(plane4[:].rearrange("p a n -> p (a n)").bitcast(I32), 0)
+        nc.vector.memset(plane8[:].rearrange("p a n -> p (a n)").bitcast(I32), 0)
+        make_identity(nc, ident[:])
+
+        def load_x(a, t0, count):
+            rows = keep.tile([P, PACK, count * P], F32, name="x_%d_%d" % (a, t0))
+            src = x[a * K_PASS:(a + 1) * K_PASS, t0 * P:(t0 + count) * P]
+            nc.sync.dma_start(out=rows[:], in_=src.rearrange("(p j) t -> p j t", j=PACK))
+            for i in range(count):
+                raw[t0 + i, a] = rows[:, :, i * P:(i + 1) * P]
+
+        def load_w4(a, n0, count):
+            words = keep.tile([P, count * 2 * NB], U8, name="w4_%d_%d" % (a, n0), align_bytes=64)
+            src = w4_words[a][:, n0 * 2 * NB:(n0 + count) * 2 * NB]
+            nc.sync.dma_start(out=words[:].bitcast(I32), in_=src.bitcast(I32))
+            for i in range(count):
+                weights[POS, a, n0 + i] = words[:, i * 2 * NB:(i + 1) * 2 * NB].bitcast(E2M1)
+
+        def load_w8(a, n):
+            words = keep.tile([P, NB], U32, name="w8_%d_%d" % (a, n), align_bytes=64)
+            src = w8_words[a].rearrange("p n i -> p (n i)")[:, n * PACK * NB:(n + 1) * PACK * NB]
+            nc.sync.dma_start(out=words[:].bitcast(I32), in_=src.bitcast(I32))
+            weights[NEG, a, n] = words[:].bitcast(E4M3)
+
+        def load_scales(plane, row, src):
+            for q in range(4):
+                nc.sync.dma_start(
+                    out=plane[32 * q + row:32 * q + row + 4, :, :].bitcast(I32),
+                    in_=src[:, 4 * q:4 * q + 4, :].rearrange("a r n -> r a n").bitcast(I32),
+                )
+
+        nc.sync.dma_start(out=b_cols[:], in_=b.rearrange("(g p c) -> p g c", g=N_BLOCKS, c=PACK))
+        load_x(0, 0, 2)
+        load_w4(0, 0, 2)
+        load_scales(plane4, 0, w4_scales)
+        load_x(0, 2, 2)
+        load_w8(0, 0)
+        load_scales(plane8, W8_ROW, w8_scales)
+        load_w8(0, 1)
+        load_x(1, 0, 2)
+        load_w4(1, 0, 2)
+        load_x(1, 2, 2)
+        load_w8(1, 0)
+        load_w8(1, 1)
+        for a in range(PASSES):
+            load_w4(a, 2, 1)
+            load_w8(a, 2)
+        for t0, count in ((4, 2), (6, 2), (8, 4)):
+            for a in range(PASSES):
+                load_x(a, t0, count)
+
+        head_groups = [(t, n) for n in range(2) for t in range(HEAD)]
+        groups = head_groups + [(t, 2) for t in range(HEAD)]
+        groups = groups + [(t, n) for t in range(HEAD, T_TILES) for n in range(N_BLOCKS)]
+        bank = {g: i % BANKS for i, g in enumerate(groups)}
+
+        bias = {}
+        spread = {}
+
+        def spread_bias(n, bank_no):
+            spread[n] = psum.tile([P, PACK, P], F32, name="spread_%d" % n, tag="bank%d" % bank_no)
+            for c in range(PACK):
+                nc.tensor.transpose(spread[n][:, c, :], b_cols[:, n, c:c + 1].to_broadcast([P, P]), ident[:])
+
+        def copy_bias(n):
+            bias[n] = keep.tile([P, NB], F32, name="bias_%d" % n)
+            nc.scalar.copy(out=bias[n][:].rearrange("p (m c) -> p m c", c=PACK), in_=spread[n][:].rearrange("p c m -> p m c"))
+
+        def rectify(on_vector, t, a, f):
+            if t not in grouped:
+                grouped[t] = stage.tile([P, len(UNITS), K_PASS], BF16, name="grouped_%d" % t, tag="grouped", align_bytes=64)
+            dst = grouped[t][:, 2 * a + f, :].rearrange("p (c i j) -> p c j i", i=4, j=PACK)
+            src = raw[t, a].rearrange("p j (c i) -> p c j i", i=4)
+            sign = 1.0 if f == POS else -1.0
+            if on_vector:
+                nc.vector.tensor_scalar(out=dst, in0=src, scalar1=sign, scalar2=0.0, op0=ALU.mult, op1=ALU.max)
+            else:
+                nc.scalar.activation(out=dst, in_=src, func=RELU, bias=zero[:], scale=sign)
+
+        def quantize(t, u0, count):
+            if t not in codes:
+                codes[t] = keep.tile([P, len(UNITS) * P], U32, name="codes_%d" % t, align_bytes=64)
+                scales[t] = keep.tile([P, len(UNITS) * P], U8, name="scales_%d" % t, align_bytes=64)
+            cols = slice(u0 * P, (u0 + count) * P)
+            nc.vector.quantize_mx(
+                out=codes[t][:, cols].bitcast(E4M3),
+                scales=scales[t][:, cols],
+                in_=grouped[t][:, u0:u0 + count, :].rearrange("p u k -> p (u k)"),
+            )
+
+        def multiply(t, n, a, f):
+            if (t, n) not in acc:
+                acc[t, n] = psum.tile([P, NB], F32, name="acc_%d_%d" % (t, n), tag="bank%d" % bank[t, n])
+            cols = slice((2 * a + f) * P, (2 * a + f + 1) * P)
+            n_cols = slice(n * NB, (n + 1) * NB)
+            w_scale = plane4[:, a, n_cols] if f == POS else plane8[W8_ROW:, a, n_cols]
+            nc.tensor.matmul_mx(
+                out=acc[t, n][:],
+                lhsT=codes[t][:, cols].bitcast(E4M3),
+                lhsT_scale=scales[t][:, cols],
+                rhs=weights[f, a, n],
+                rhs_scale=w_scale,
+                start=(a, f) == UNITS[0],
+                stop=(a, f) == UNITS[-1],
+            )
+
+        def add_bias(t, n):
+            if t not in result:
+                result[t] = keep.tile([P, M], F32, name="result_%d" % t)
+            nc.vector.tensor_tensor(out=result[t][:, n * NB:(n + 1) * NB], in0=acc[t, n][:], in1=bias[n][:], op=ALU.add)
+
+        def store(t, n0, count):
+            cols = slice(n0 * NB, (n0 + count) * NB)
+            nc.sync.dma_start(out=out[t * P:(t + 1) * P, cols], in_=result[t][:, cols])
+
+        def prepare_shared(t, a):
+            rectify(True, t, a, POS)
+            rectify(False, t, a, NEG)
+
+        def prepare_pair(t0, a):
+            rectify(True, t0, a, POS)
+            rectify(False, t0, a, NEG)
+            rectify(True, t0 + 1, a, POS)
+            rectify(False, t0 + 1, a, NEG)
+            quantize(t0, 2 * a + POS, 1)
+            quantize(t0 + 1, 2 * a + POS, 1)
+            quantize(t0, 2 * a + NEG, 1)
+            quantize(t0 + 1, 2 * a + NEG, 1)
+
+        def rectify_tile(t):
+            for a, f in UNITS:
+                rectify(False, t, a, f)
+
+        for n, g in enumerate(((3, 0), (2, 1), (3, 1))):
+            spread_bias(n, bank[g])
+        prepare_pair(0, 0)
+        copy_bias(0)
+        copy_bias(1)
+        copy_bias(2)
+        prepare_pair(2, 0)
+        prepare_pair(0, 1)
+        prepare_pair(2, 1)
+        for a in range(PASSES):
+            for t in range(HEAD):
+                for n in range(2):
+                    multiply(t, n, a, POS)
+            for t, n in head_groups:
+                multiply(t, n, a, NEG)
+        rectify_tile(HEAD)
+        for t, n in head_groups:
+            add_bias(t, n)
+        quantize(HEAD, 0, len(UNITS))
+        rectify_tile(HEAD + 1)
+        for t in range(HEAD):
+            for a, f in UNITS:
+                multiply(t, 2, a, f)
+            add_bias(t, 2)
+            store(t, 0, N_BLOCKS)
+            if t == 1:
+                quantize(HEAD + 1, 0, len(UNITS))
+        for t in range(HEAD, T_TILES):
+            if t + 2 < T_TILES:
+                rectify_tile(t + 2)
+            for n in range(N_BLOCKS):
+                for a, f in UNITS:
+                    multiply(t, n, a, f)
+                add_bias(t, n)
+                if n == 1 and t + 2 < T_TILES:
+                    quantize(t + 2, 0, len(UNITS))
+                if t >= T_TILES - 2:
+                    store(t, n, 1)
+            if t < T_TILES - 2:
+                store(t, 0, N_BLOCKS)

@@ -53,7 +53,7 @@ def tile_mix_feat_tm_crelu_bias_kernel(tc, x, w4_words, w4_scales, w8_words, w8_
         ident = keep.tile([P, P], F32, name="ident")
         b_cols = keep.tile([P, N_BLOCKS, PACK], F32, name="b_cols")
 
-        nc.vector.memset(zero_in[:], 0.0)
+        nc.gpsimd.memset(zero_in[:], 0.0)
         nc.scalar.activation(out=zero[:], in_=zero_in[:], func=RELU, bias=zero_in[:])
         nc.vector.memset(plane4[:].rearrange("p a n -> p (a n)").bitcast(I32), 0)
         nc.vector.memset(plane8[:].rearrange("p a n -> p (a n)").bitcast(I32), 0)
@@ -71,19 +71,19 @@ def tile_mix_feat_tm_crelu_bias_kernel(tc, x, w4_words, w4_scales, w8_words, w8_
             src = w4_words[a][:, n0 * 2 * NB:(n0 + count) * 2 * NB]
             nc.sync.dma_start(out=words[:].bitcast(I32), in_=src.bitcast(I32))
             for i in range(count):
-                weights[POS, a, n0 + i] = words[:, i * 2 * NB:(i + 1) * 2 * NB].bitcast(E2M1)
+                weights[POS, a, n0 + i] = words[:, i * 2 * NB:(i + 1) * 2 * NB]
 
         def load_w8(a, n):
             words = keep.tile([P, NB], U32, name="w8_%d_%d" % (a, n), align_bytes=64)
             src = w8_words[a].rearrange("p n i -> p (n i)")[:, n * PACK * NB:(n + 1) * PACK * NB]
             nc.sync.dma_start(out=words[:].bitcast(I32), in_=src.bitcast(I32))
-            weights[NEG, a, n] = words[:].bitcast(E4M3)
+            weights[NEG, a, n] = words[:]
 
         def load_scales(plane, row, src):
-            for q in range(4):
+            for r in range(4):
                 nc.sync.dma_start(
-                    out=plane[32 * q + row:32 * q + row + 4, :, :].bitcast(I32),
-                    in_=src[:, 4 * q:4 * q + 4, :].rearrange("a r n -> r a n").bitcast(I32),
+                    out=plane[row + r:P:32, :, :].bitcast(I32),
+                    in_=src.rearrange("a (q r) n -> r q a n", r=4)[r].bitcast(I32),
                 )
 
         nc.sync.dma_start(out=b_cols[:], in_=b.rearrange("(g p c) -> p g c", g=N_BLOCKS, c=PACK))
@@ -145,29 +145,36 @@ def tile_mix_feat_tm_crelu_bias_kernel(tc, x, w4_words, w4_scales, w8_words, w8_
                 in_=grouped[t][:, u0:u0 + count, :].rearrange("p u k -> p (u k)"),
             )
 
-        def multiply(t, n, a, f):
-            if (t, n) not in acc:
-                acc[t, n] = psum.tile([P, NB], F32, name="acc_%d_%d" % (t, n), tag="bank%d" % bank[t, n])
+        def multiply(t, n, a, f, c0=0, width=NB):
+            if (t, n, c0) not in acc:
+                bank_no = (bank[t, n] + c0 // width) % BANKS
+                acc[t, n, c0] = psum.tile([P, width], F32, name="acc_%d_%d_%d" % (t, n, c0), tag="bank%d" % bank_no)
             cols = slice((2 * a + f) * P, (2 * a + f + 1) * P)
-            n_cols = slice(n * NB, (n + 1) * NB)
-            w_scale = plane4[:, a, n_cols] if f == POS else plane8[W8_ROW:, a, n_cols]
+            n_cols = slice(n * NB + c0, n * NB + c0 + width)
+            if f == POS:
+                w_words = weights[f, a, n][:, 2 * c0:2 * (c0 + width)].bitcast(E2M1)
+                w_scale = plane4[:, a, n_cols]
+            else:
+                w_words = weights[f, a, n][:, c0:c0 + width].bitcast(E4M3)
+                w_scale = plane8[W8_ROW:, a, n_cols]
             nc.tensor.matmul_mx(
-                out=acc[t, n][:],
+                out=acc[t, n, c0][:],
                 lhsT=codes[t][:, cols].bitcast(E4M3),
                 lhsT_scale=scales[t][:, cols],
-                rhs=weights[f, a, n],
+                rhs=w_words,
                 rhs_scale=w_scale,
                 start=(a, f) == UNITS[0],
                 stop=(a, f) == UNITS[-1],
             )
 
-        def add_bias(t, n):
+        def add_bias(t, n, c0=0, width=NB):
             if t not in result:
                 result[t] = keep.tile([P, M], F32, name="result_%d" % t)
-            nc.vector.tensor_tensor(out=result[t][:, n * NB:(n + 1) * NB], in0=acc[t, n][:], in1=bias[n][:], op=ALU.add)
+            n_cols = slice(n * NB + c0, n * NB + c0 + width)
+            nc.vector.tensor_tensor(out=result[t][:, n_cols], in0=acc[t, n, c0][:], in1=bias[n][:, c0:c0 + width], op=ALU.add)
 
-        def store(t, n0, count):
-            cols = slice(n0 * NB, (n0 + count) * NB)
+        def store(t, c0, width):
+            cols = slice(c0, c0 + width)
             nc.sync.dma_start(out=out[t * P:(t + 1) * P, cols], in_=result[t][:, cols])
 
         def prepare_shared(t, a):
@@ -197,12 +204,19 @@ def tile_mix_feat_tm_crelu_bias_kernel(tc, x, w4_words, w4_scales, w8_words, w8_
         prepare_pair(2, 0)
         prepare_pair(0, 1)
         prepare_pair(2, 1)
-        for a in range(PASSES):
-            for t in range(HEAD):
+        for t in range(HEAD):
+            for n in range(2):
+                multiply(t, n, 0, POS)
+        for t, n in head_groups:
+            multiply(t, n, 0, NEG)
+        for t0 in (0, 2):
+            for t in (t0, t0 + 1):
                 for n in range(2):
-                    multiply(t, n, a, POS)
-            for t, n in head_groups:
-                multiply(t, n, a, NEG)
+                    multiply(t, n, 1, POS)
+            for t in (t0, t0 + 1):
+                multiply(t, 0, 1, NEG)
+        for t in range(HEAD):
+            multiply(t, 1, 1, NEG)
         rectify_tile(HEAD)
         for t, n in head_groups:
             add_bias(t, n)
@@ -212,19 +226,28 @@ def tile_mix_feat_tm_crelu_bias_kernel(tc, x, w4_words, w4_scales, w8_words, w8_
             for a, f in UNITS:
                 multiply(t, 2, a, f)
             add_bias(t, 2)
-            store(t, 0, N_BLOCKS)
+            store(t, 0, M)
             if t == 1:
                 quantize(HEAD + 1, 0, len(UNITS))
         for t in range(HEAD, T_TILES):
             if t + 2 < T_TILES:
                 rectify_tile(t + 2)
             for n in range(N_BLOCKS):
+                if (t, n) == groups[-1]:
+                    break
                 for a, f in UNITS:
                     multiply(t, n, a, f)
                 add_bias(t, n)
                 if n == 1 and t + 2 < T_TILES:
                     quantize(t + 2, 0, len(UNITS))
                 if t >= T_TILES - 2:
-                    store(t, n, 1)
+                    store(t, n * NB, NB)
             if t < T_TILES - 2:
-                store(t, 0, N_BLOCKS)
+                store(t, 0, M)
+        t, n = groups[-1]
+        for c0 in range(0, NB, P):
+            for a, f in UNITS:
+                multiply(t, n, a, f, c0, P)
+            add_bias(t, n, c0, P)
+            if c0 % (2 * P):
+                store(t, n * NB + c0 - P, 2 * P)

@@ -126,8 +126,8 @@ def tile_mix_feat_tm_crelu_bias_kernel(tc, x, w4_words, w4_scales, w8_words, w8_
         def rectify(on_vector, t, a, f):
             if t not in grouped:
                 grouped[t] = stage.tile([P, len(UNITS), K_PASS], BF16, name="grouped_%d" % t, tag="grouped", align_bytes=64)
-            dst = grouped[t][:, 2 * a + f, :].rearrange("p (c i j) -> p c j i", i=4, j=PACK)
-            src = raw[t, a].rearrange("p j (c i) -> p c j i", i=4)
+            dst = grouped[t][:, 2 * a + f, :].rearrange("p (c j) -> p c j", j=PACK)
+            src = raw[t, a].rearrange("p j c -> p c j")
             sign = 1.0 if f == POS else -1.0
             if on_vector:
                 nc.vector.tensor_scalar(out=dst, in0=src, scalar1=sign, scalar2=0.0, op0=ALU.mult, op1=ALU.max)
@@ -192,7 +192,7 @@ def tile_mix_feat_tm_crelu_bias_kernel(tc, x, w4_words, w4_scales, w8_words, w8_
             quantize(t0 + 1, 2 * a + NEG, 1)
 
         def rectify_tile(t):
-            for a, f in UNITS:
+            for a, f in UNITS[1:]:
                 rectify(False, t, a, f)
 
         for n, g in enumerate(((3, 0), (2, 1), (3, 1))):
@@ -218,10 +218,14 @@ def tile_mix_feat_tm_crelu_bias_kernel(tc, x, w4_words, w4_scales, w8_words, w8_
         for t in range(HEAD):
             multiply(t, 1, 1, NEG)
         rectify_tile(HEAD)
-        for t, n in head_groups:
+        rectify_tile(HEAD + 1)
+        for t, n in head_groups[:-2]:
+            add_bias(t, n)
+        rectify(True, HEAD, 0, POS)
+        rectify(True, HEAD + 1, 0, POS)
+        for t, n in head_groups[-2:]:
             add_bias(t, n)
         quantize(HEAD, 0, len(UNITS))
-        rectify_tile(HEAD + 1)
         for t in range(HEAD):
             for a, f in UNITS:
                 multiply(t, 2, a, f)
@@ -238,6 +242,8 @@ def tile_mix_feat_tm_crelu_bias_kernel(tc, x, w4_words, w4_scales, w8_words, w8_
                 for a, f in UNITS:
                     multiply(t, n, a, f)
                 add_bias(t, n)
+                if n == 0 and t + 2 < T_TILES:
+                    rectify(True, t + 2, 0, POS)
                 if n == 1 and t + 2 < T_TILES:
                     quantize(t + 2, 0, len(UNITS))
                 if t >= T_TILES - 2:

@@ -45,6 +45,7 @@ def tile_mix_feat_tm_crelu_bias_kernel(tc, x, w4_words, w4_scales, w8_words, w8_
         scales = {}
         acc = {}
         result = {}
+        passes_done = {}
 
         plane4 = keep.tile([P, PASSES, M], U8, name="plane4", align_bytes=64)
         plane8 = keep.tile([P, PASSES, M], U8, name="plane8", align_bytes=64)
@@ -101,6 +102,7 @@ def tile_mix_feat_tm_crelu_bias_kernel(tc, x, w4_words, w4_scales, w8_words, w8_
         load_w8(1, 1)
         for a in range(PASSES):
             load_w4(a, 2, 1)
+        for a in range(PASSES):
             load_w8(a, 2)
         for t0, count in ((4, 2), (6, 2), (8, 4)):
             for a in range(PASSES):
@@ -147,6 +149,7 @@ def tile_mix_feat_tm_crelu_bias_kernel(tc, x, w4_words, w4_scales, w8_words, w8_
 
         def multiply(t, n, a, f, c0=0, width=NB):
             if (t, n, c0) not in acc:
+                passes_done[t, n, c0] = 0
                 bank_no = (bank[t, n] + c0 // width) % BANKS
                 acc[t, n, c0] = psum.tile([P, width], F32, name="acc_%d_%d_%d" % (t, n, c0), tag="bank%d" % bank_no)
             cols = slice((2 * a + f) * P, (2 * a + f + 1) * P)
@@ -163,9 +166,10 @@ def tile_mix_feat_tm_crelu_bias_kernel(tc, x, w4_words, w4_scales, w8_words, w8_
                 lhsT_scale=scales[t][:, cols],
                 rhs=w_words,
                 rhs_scale=w_scale,
-                start=(a, f) == UNITS[0],
-                stop=(a, f) == UNITS[-1],
+                start=passes_done[t, n, c0] == 0,
+                stop=passes_done[t, n, c0] == len(UNITS) - 1,
             )
+            passes_done[t, n, c0] += 1
 
         def add_bias(t, n, c0=0, width=NB):
             if t not in result:
@@ -194,6 +198,14 @@ def tile_mix_feat_tm_crelu_bias_kernel(tc, x, w4_words, w4_scales, w8_words, w8_
         def rectify_tile(t):
             for a, f in UNITS[1:]:
                 rectify(False, t, a, f)
+
+        def formats(i):
+            return (POS, NEG) if i % 2 == 0 else (NEG, POS)
+
+        def multiply_group(t, n, i, c0=0, width=NB):
+            for f in formats(i):
+                for a in range(PASSES):
+                    multiply(t, n, a, f, c0, width)
 
         for n, g in enumerate(((3, 0), (2, 1), (3, 1))):
             spread_bias(n, bank[g])
@@ -227,33 +239,32 @@ def tile_mix_feat_tm_crelu_bias_kernel(tc, x, w4_words, w4_scales, w8_words, w8_
             add_bias(t, n)
         quantize(HEAD, 0, len(UNITS))
         for t in range(HEAD):
-            for a, f in UNITS:
-                multiply(t, 2, a, f)
+            multiply_group(t, 2, t)
             add_bias(t, 2)
             store(t, 0, M)
             if t == 1:
                 quantize(HEAD + 1, 0, len(UNITS))
-        for t in range(HEAD, T_TILES):
-            if t + 2 < T_TILES:
-                rectify_tile(t + 2)
+        for t in range(HEAD, T_TILES - 2):
+            rectify_tile(t + 2)
+            rectify(True, t + 2, 0, POS)
+            first, second = formats(t)
             for n in range(N_BLOCKS):
-                if (t, n) == groups[-1]:
-                    break
-                for a, f in UNITS:
-                    multiply(t, n, a, f)
+                for a in range(PASSES):
+                    multiply(t, n, a, first)
+            for n in range(N_BLOCKS):
+                for a in range(PASSES):
+                    multiply(t, n, a, second)
                 add_bias(t, n)
-                if n == 0 and t + 2 < T_TILES:
-                    rectify(True, t + 2, 0, POS)
-                if n == 1 and t + 2 < T_TILES:
+                if n == 0:
                     quantize(t + 2, 0, len(UNITS))
-                if t >= T_TILES - 2:
-                    store(t, n * NB, NB)
-            if t < T_TILES - 2:
-                store(t, 0, M)
+            store(t, 0, M)
+        for i, (t, n) in enumerate(groups[-6:-1]):
+            multiply_group(t, n, i)
+            add_bias(t, n)
+            store(t, n * NB, NB)
         t, n = groups[-1]
         for c0 in range(0, NB, P):
-            for a, f in UNITS:
-                multiply(t, n, a, f, c0, P)
+            multiply_group(t, n, 1 + c0 // P, c0, P)
             add_bias(t, n, c0, P)
             if c0 % (2 * P):
                 store(t, n * NB + c0 - P, 2 * P)

@@ -56,8 +56,8 @@ def tile_mix_feat_tm_crelu_bias_kernel(tc, x, w4_words, w4_scales, w8_words, w8_
 
         nc.gpsimd.memset(zero_in[:], 0.0)
         nc.scalar.activation(out=zero[:], in_=zero_in[:], func=RELU, bias=zero_in[:])
-        nc.vector.memset(plane4[:].rearrange("p a n -> p (a n)").bitcast(I32), 0)
         nc.vector.memset(plane8[:].rearrange("p a n -> p (a n)").bitcast(I32), 0)
+        nc.vector.memset(plane4[:].rearrange("p a n -> p (a n)").bitcast(I32), 0)
         make_identity(nc, ident[:])
 
         def load_x(a, t0, count):
@@ -80,20 +80,23 @@ def tile_mix_feat_tm_crelu_bias_kernel(tc, x, w4_words, w4_scales, w8_words, w8_
             nc.sync.dma_start(out=words[:].bitcast(I32), in_=src.bitcast(I32))
             weights[NEG, a, n] = words[:]
 
-        def load_scales(plane, row, src):
-            for r in range(4):
-                nc.sync.dma_start(
-                    out=plane[row + r:P:32, :, :].bitcast(I32),
-                    in_=src.rearrange("a (q r) n -> r q a n", r=4)[r].bitcast(I32),
-                )
+        def load_scales(queue, plane, row, src, r):
+            queue.dma_start(
+                out=plane[row + r:P:32, :, :].bitcast(I32),
+                in_=src.rearrange("a (q r) n -> r q a n", r=4)[r].bitcast(I32),
+            )
 
+        for r in range(2, 4):
+            load_scales(nc.gpsimd, plane8, W8_ROW, w8_scales, r)
         nc.sync.dma_start(out=b_cols[:], in_=b.rearrange("(g p c) -> p g c", g=N_BLOCKS, c=PACK))
         load_x(0, 0, 2)
         load_w4(0, 0, 2)
-        load_scales(plane4, 0, w4_scales)
+        for r in range(4):
+            load_scales(nc.sync, plane4, 0, w4_scales, r)
+            if r < 2:
+                load_scales(nc.sync, plane8, W8_ROW, w8_scales, r)
         load_x(0, 2, 2)
         load_w8(0, 0)
-        load_scales(plane8, W8_ROW, w8_scales)
         load_w8(0, 1)
         load_x(1, 0, 2)
         load_w4(1, 0, 2)

from contextlib import ExitStack

import concourse.mybir as mybir
from concourse.masks import make_identity

K, M, T = 1024, 1536, 1536
FLOPS = 2 * 2 * K * M * T

F32 = mybir.dt.float32
BF16 = mybir.dt.bfloat16
I32 = mybir.dt.int32
U32 = mybir.dt.uint32
U8 = mybir.dt.uint8
E4M3 = mybir.dt.float8_e4m3fn_x4
E2M1 = mybir.dt.float4_e2m1fn_x4
ALU = mybir.AluOpType
RELU = mybir.ActivationFunctionType.Relu

P = 128
PACK = 4
K_PASS = P * PACK
PASSES = K // K_PASS
NB = 512
N_BLOCKS = M // NB
T_TILES = T // P
BANKS = 8
HEAD = 4
POS, NEG = 0, 1
UNITS = [(a, f) for a in range(PASSES) for f in (POS, NEG)]
W8_ROW = 4


def tile_mix_feat_tm_crelu_bias_kernel(tc, x, w4_words, w4_scales, w8_words, w8_scales, b, out):
    nc = tc.nc
    with ExitStack() as ctx:
        keep = ctx.enter_context(tc.tile_pool(name="keep", bufs=1))
        stage = ctx.enter_context(tc.tile_pool(name="stage", bufs=6))
        psum = ctx.enter_context(tc.psum_pool(name="psum", bufs=1))
        ctx.enter_context(tc.manual_schedule())

        raw = {}
        weights = {}
        grouped = {}
        codes = {}
        scales = {}
        acc = {}
        result = {}
        passes_done = {}

        plane4 = keep.tile([P, PASSES, M], U8, name="plane4", align_bytes=64)
        plane8 = keep.tile([P, PASSES, M], U8, name="plane8", align_bytes=64)
        zero_in = keep.tile([P, 1], F32, name="zero_in")
        zero = keep.tile([P, 1], F32, name="zero")
        ident = keep.tile([P, P], F32, name="ident")
        b_cols = keep.tile([P, N_BLOCKS, PACK], F32, name="b_cols")

        nc.gpsimd.memset(zero_in[:], 0.0)
        nc.scalar.activation(out=zero[:], in_=zero_in[:], func=RELU, bias=zero_in[:])
        nc.vector.memset(plane8[:].rearrange("p a n -> p (a n)").bitcast(I32), 0)
        nc.vector.memset(plane4[:].rearrange("p a n -> p (a n)").bitcast(I32), 0)
        make_identity(nc, ident[:])

        def load_x(a, t0, count):
            rows = keep.tile([P, PACK, count * P], F32, name="x_%d_%d" % (a, t0))
            src = x[a * K_PASS:(a + 1) * K_PASS, t0 * P:(t0 + count) * P]
            nc.sync.dma_start(out=rows[:], in_=src.rearrange("(p j) t -> p j t", j=PACK))
            for i in range(count):
                raw[t0 + i, a] = rows[:, :, i * P:(i + 1) * P]

        def load_w4(a, n0, count):
            words = keep.tile([P, count * 2 * NB], U8, name="w4_%d_%d" % (a, n0), align_bytes=64)
            src = w4_words[a][:, n0 * 2 * NB:(n0 + count) * 2 * NB]
            nc.sync.dma_start(out=words[:].bitcast(I32), in_=src.bitcast(I32))
            for i in range(count):
                weights[POS, a, n0 + i] = words[:, i * 2 * NB:(i + 1) * 2 * NB]

        def load_w8(a, n):
            words = keep.tile([P, NB], U32, name="w8_%d_%d" % (a, n), align_bytes=64)
            src = w8_words[a].rearrange("p n i -> p (n i)")[:, n * PACK * NB:(n + 1) * PACK * NB]
            nc.sync.dma_start(out=words[:].bitcast(I32), in_=src.bitcast(I32))
            weights[NEG, a, n] = words[:]

        def load_scales(queue, plane, row, src, r):
            queue.dma_start(
                out=plane[row + r:P:32, :, :].bitcast(I32),
                in_=src.rearrange("a (q r) n -> r q a n", r=4)[r].bitcast(I32),
            )

        for r in range(2, 4):
            load_scales(nc.gpsimd, plane8, W8_ROW, w8_scales, r)
        nc.sync.dma_start(out=b_cols[:], in_=b.rearrange("(g p c) -> p g c", g=N_BLOCKS, c=PACK))
        load_x(0, 0, 2)
        load_w4(0, 0, 2)
        for r in range(4):
            load_scales(nc.sync, plane4, 0, w4_scales, r)
            if r < 2:
                load_scales(nc.sync, plane8, W8_ROW, w8_scales, r)
        load_x(0, 2, 2)
        load_w8(0, 0)
        load_w8(0, 1)
        load_x(1, 0, 2)
        load_w4(1, 0, 2)
        load_x(1, 2, 2)
        load_w8(1, 0)
        load_w8(1, 1)
        for a in range(PASSES):
            load_w4(a, 2, 1)
        for a in range(PASSES):
            load_w8(a, 2)
        for t0, count in ((4, 2), (6, 2), (8, 4)):
            for a in range(PASSES):
                load_x(a, t0, count)

        head_groups = [(t, n) for n in range(2) for t in range(HEAD)]
        groups = head_groups + [(t, 2) for t in range(HEAD)]
        groups = groups + [(t, n) for t in range(HEAD, T_TILES) for n in range(N_BLOCKS)]
        bank = {g: i % BANKS for i, g in enumerate(groups)}

        bias = {}
        spread = {}

        def spread_bias(n, bank_no):
            spread[n] = psum.tile([P, PACK, P], F32, name="spread_%d" % n, tag="bank%d" % bank_no)
            for c in range(PACK):
                nc.tensor.transpose(spread[n][:, c, :], b_cols[:, n, c:c + 1].to_broadcast([P, P]), ident[:])

        def copy_bias(n):
            bias[n] = keep.tile([P, NB], F32, name="bias_%d" % n)
            nc.scalar.copy(out=bias[n][:].rearrange("p (m c) -> p m c", c=PACK), in_=spread[n][:].rearrange("p c m -> p m c"))

        def rectify(on_vector, t, a, f):
            if t not in grouped:
                grouped[t] = stage.tile([P, len(UNITS), K_PASS], BF16, name="grouped_%d" % t, tag="grouped", align_bytes=64)
            dst = grouped[t][:, 2 * a + f, :].rearrange("p (c j) -> p c j", j=PACK)
            src = raw[t, a].rearrange("p j c -> p c j")
            sign = 1.0 if f == POS else -1.0
            if on_vector:
                nc.vector.tensor_scalar(out=dst, in0=src, scalar1=sign, scalar2=0.0, op0=ALU.mult, op1=ALU.max)
            else:
                nc.scalar.activation(out=dst, in_=src, func=RELU, bias=zero[:], scale=sign)

        def quantize(t, u0, count):
            if t not in codes:
                codes[t] = keep.tile([P, len(UNITS) * P], U32, name="codes_%d" % t, align_bytes=64)
                scales[t] = keep.tile([P, len(UNITS) * P], U8, name="scales_%d" % t, align_bytes=64)
            cols = slice(u0 * P, (u0 + count) * P)
            nc.vector.quantize_mx(
                out=codes[t][:, cols].bitcast(E4M3),
                scales=scales[t][:, cols],
                in_=grouped[t][:, u0:u0 + count, :].rearrange("p u k -> p (u k)"),
            )

        def multiply(t, n, a, f, c0=0, width=NB):
            if (t, n, c0) not in acc:
                passes_done[t, n, c0] = 0
                bank_no = (bank[t, n] + c0 // width) % BANKS
                acc[t, n, c0] = psum.tile([P, width], F32, name="acc_%d_%d_%d" % (t, n, c0), tag="bank%d" % bank_no)
            cols = slice((2 * a + f) * P, (2 * a + f + 1) * P)
            n_cols = slice(n * NB + c0, n * NB + c0 + width)
            if f == POS:
                w_words = weights[f, a, n][:, 2 * c0:2 * (c0 + width)].bitcast(E2M1)
                w_scale = plane4[:, a, n_cols]
            else:
                w_words = weights[f, a, n][:, c0:c0 + width].bitcast(E4M3)
                w_scale = plane8[W8_ROW:, a, n_cols]
            nc.tensor.matmul_mx(
                out=acc[t, n, c0][:],
                lhsT=codes[t][:, cols].bitcast(E4M3),
                lhsT_scale=scales[t][:, cols],
                rhs=w_words,
                rhs_scale=w_scale,
                start=passes_done[t, n, c0] == 0,
                stop=passes_done[t, n, c0] == len(UNITS) - 1,
            )
            passes_done[t, n, c0] += 1

        def add_bias(t, n, c0=0, width=NB):
            if t not in result:
                result[t] = keep.tile([P, M], F32, name="result_%d" % t)
            n_cols = slice(n * NB + c0, n * NB + c0 + width)
            nc.vector.tensor_tensor(out=result[t][:, n_cols], in0=acc[t, n, c0][:], in1=bias[n][:, c0:c0 + width], op=ALU.add)

        def store(t, c0, width):
            cols = slice(c0, c0 + width)
            nc.sync.dma_start(out=out[t * P:(t + 1) * P, cols], in_=result[t][:, cols])

        def prepare_shared(t, a):
            rectify(True, t, a, POS)
            rectify(False, t, a, NEG)

        def prepare_pair(t0, a):
            rectify(True, t0, a, POS)
            rectify(False, t0, a, NEG)
            rectify(True, t0 + 1, a, POS)
            rectify(False, t0 + 1, a, NEG)
            quantize(t0, 2 * a + POS, 1)
            quantize(t0 + 1, 2 * a + POS, 1)
            quantize(t0, 2 * a + NEG, 1)
            quantize(t0 + 1, 2 * a + NEG, 1)

        def rectify_tile(t):
            for a, f in UNITS[1:]:
                rectify(False, t, a, f)

        def formats(i):
            return (POS, NEG) if i % 2 == 0 else (NEG, POS)

        def multiply_group(t, n, i, c0=0, width=NB):
            for f in formats(i):
                for a in range(PASSES):
                    multiply(t, n, a, f, c0, width)

        for n, g in enumerate(((3, 0), (2, 1), (3, 1))):
            spread_bias(n, bank[g])
        prepare_pair(0, 0)
        copy_bias(0)
        copy_bias(1)
        copy_bias(2)
        prepare_pair(2, 0)
        prepare_pair(0, 1)
        prepare_pair(2, 1)
        for t in range(HEAD):
            for n in range(2):
                multiply(t, n, 0, POS)
        for t, n in head_groups:
            multiply(t, n, 0, NEG)
        for t0 in (0, 2):
            for t in (t0, t0 + 1):
                for n in range(2):
                    multiply(t, n, 1, POS)
            for t in (t0, t0 + 1):
                multiply(t, 0, 1, NEG)
        for t in range(HEAD):
            multiply(t, 1, 1, NEG)
        rectify_tile(HEAD)
        rectify_tile(HEAD + 1)
        for t, n in head_groups[:-2]:
            add_bias(t, n)
        rectify(True, HEAD, 0, POS)
        rectify(True, HEAD + 1, 0, POS)
        for t, n in head_groups[-2:]:
            add_bias(t, n)
        quantize(HEAD, 0, len(UNITS))
        for t in range(HEAD):
            multiply_group(t, 2, t)
            add_bias(t, 2)
            store(t, 0, M)
            if t == 1:
                quantize(HEAD + 1, 0, len(UNITS))
        for t in range(HEAD, T_TILES - 2):
            rectify_tile(t + 2)
            rectify(True, t + 2, 0, POS)
            first, second = formats(t)
            for n in range(N_BLOCKS):
                for a in range(PASSES):
                    multiply(t, n, a, first)
            for n in range(N_BLOCKS):
                for a in range(PASSES):
                    multiply(t, n, a, second)
                add_bias(t, n)
                if n == 0:
                    quantize(t + 2, 0, len(UNITS))
            store(t, 0, M)
        for i, (t, n) in enumerate(groups[-6:-1]):
            multiply_group(t, n, i)
            add_bias(t, n)
            store(t, n * NB, NB)
        t, n = groups[-1]
        for c0 in range(0, NB, P):
            multiply_group(t, n, 1 + c0 // P, c0, P)
            add_bias(t, n, c0, P)
            if c0 % (2 * P):
                store(t, n * NB + c0 - P, 2 * P)
